import numpy as np
import ml_dtypes


def mxq(x, axis, fmt="e4m3"):
    dtype, down = {"e4m3": (ml_dtypes.float8_e4m3fn, 7), "e5m2": (ml_dtypes.float8_e5m2, 14)}[fmt]
    v = np.moveaxis(np.asarray(x, np.float32).astype(ml_dtypes.bfloat16).astype(np.float64), axis, -1)
    blocks = v.reshape(v.shape[:-1] + (-1, 32))
    amax = np.abs(blocks).max(-1, keepdims=True)
    byte = np.maximum(np.where(amax > 0, np.frexp(amax)[1] - 1 + 127, 0) - down, 1)
    scale = np.exp2(byte - 127.0)
    codes = (blocks / scale).astype(np.float32).astype(dtype).astype(np.float64)
    return np.moveaxis((codes * scale).reshape(v.shape), -1, axis)


WIDE = False


def mx_kscale(k):
    if not WIDE:
        return np.ones(k)
    levels = np.array([10, -10, 5, -5, 0])
    if k % 512:
        return np.exp2(np.random.permutation(np.resize(levels, k // 32))).repeat(32)
    a = np.empty((k // 512, 16))
    for p in range(k // 512):
        a[p, :8] = np.random.permutation(np.resize(levels, 8))
        for g in range(8):
            far = levels[np.abs(levels - a[p, g]) >= 10]
            a[p, g + 8] = far[np.random.randint(len(far))]
    return np.exp2(a.ravel()).repeat(32)


def f64(x):
    return np.asarray(x).astype(np.float64)


def striped(idx):
    return np.tile(idx.reshape(-1, 16).T, (8, 1)).astype(np.uint16)


def unstriped(offs):
    return offs[:16].T.reshape(-1).astype(np.int64)


def pack_weight(w):
    k, n = w.shape
    w = f64(np.asarray(w, np.float32).astype(ml_dtypes.bfloat16)).reshape(k // 32, 32, n)
    amax = np.abs(w).max(1)
    byte = np.clip(np.where(amax > 0, np.frexp(amax)[1] - 1 + 127 - 7, 1), 1, 254)
    scaled = (w * np.exp2(127.0 - byte)[:, None, :]).reshape(k, n).astype(np.float32)
    words = np.ascontiguousarray(scaled.reshape(k // 512, 128, 4, n).transpose(0, 1, 3, 2)).astype(ml_dtypes.float8_e4m3fn).view(np.uint8)
    return words, np.ascontiguousarray(byte.astype(np.uint8).reshape(k // 512, 16, n))


def unpack_weight(words, scales):
    g, p, n, _ = words.shape
    vals = np.ascontiguousarray(words).view(ml_dtypes.float8_e4m3fn).astype(np.float64) * np.repeat(np.exp2(scales.astype(np.float64) - 127.0), 8, axis=1)[..., None]
    return vals.transpose(0, 1, 3, 2).reshape(g * 512, n)


K, T, S, N, W = 512, 2048, 256, 512, 128


def setup_inputs():
    n = np.random.standard_normal
    s = mx_kscale(K)[:, None]
    packed_xT = pack_weight(n((K, T)) * s)
    perm = np.random.permutation(S)
    return {
        "x_words": packed_xT[0],
        "x_scales": packed_xT[1],
        "w1": (n((K, N)) / np.sqrt(2 * K) / s).astype(np.float32),
        "w2": (n((K, N)) / np.sqrt(2 * K) / s).astype(np.float32),
        "offs": striped(np.random.permutation(T)[:S]),
        "two": striped(np.random.permutation(T)[:S]),
        "n1": striped(perm[:W]),
        "n2": striped(perm[W:]),
    }


def reference(x_words, x_scales, w1, w2, offs, two, n1, n2):
    xq = unpack_weight(x_words, x_scales)[:, unstriped(offs)]
    x_two = unpack_weight(x_words, x_scales)[:, unstriped(two)]
    h = mxq(f64(w1), 0, "e4m3").T @ xq + mxq(f64(w2), 0, "e4m3").T @ x_two
    pb = h[:, unstriped(n2)]
    pa = h[:, unstriped(n1)]
    rb = pb - (0.5 * pa)
    ra = np.sqrt((pa) ** 2 + (pb) ** 2 + 0.25)
    ds = np.zeros((N, S))
    ds[:, unstriped(n1)] = ra
    out = ds.copy()
    out[:, unstriped(n2)] = rb
    return out

@@ -1,0 +1,160 @@
+from contextlib import ExitStack
+
+import concourse.mybir as mybir
+
+K, T, S, N, W = 512, 2048, 256, 512, 128
+FLOPS = 2 * 2 * K * N * S
+
+F32 = mybir.dt.float32
+BF16 = mybir.dt.bfloat16
+I32 = mybir.dt.int32
+U32 = mybir.dt.uint32
+U16 = mybir.dt.uint16
+U8 = mybir.dt.uint8
+FP8X4 = mybir.dt.float8_e4m3fn_x4
+ACT = mybir.ActivationFunctionType
+ALU = mybir.AluOpType
+
+P = 128
+PACK = 4
+BLOCKS = N // P
+
+
+def interleave(engine_copy, grouped, raw):
+    engine_copy(
+        out=grouped.rearrange("p (c i t) -> p c t i", i=4, t=PACK),
+        in_=raw.rearrange("p t (c i) -> p c t i", i=4),
+    )
+
+
+def tile_picked_ottpolar_none_p_kernel(tc, x_words, x_scales, w1, w2, offs, two, n1, n2, out):
+    nc = tc.nc
+    with ExitStack() as ctx:
+        keep = ctx.enter_context(tc.tile_pool(name="keep", bufs=1))
+        turns = ctx.enter_context(tc.tile_pool(name="turns", bufs=1))
+        psum = ctx.enter_context(tc.psum_pool(name="psum", bufs=1))
+
+        chunks = [(0, 128), (128, 128), (256, 256)]
+        raw = {}
+
+        def load(name, w, c, queue):
+            start, width = chunks[c]
+            tile = keep.tile([P, PACK, width], F32, name="raw_%s_%d" % (name, c))
+            queue.dma_start(out=tile[:], in_=w.rearrange("(p j) m -> p j m", j=PACK)[:, :, start : start + width])
+            raw[name, c] = tile
+
+        load("w1", w1, 0, nc.sync)
+        offs_sb = keep.tile([P, S // 16], U16, name="offs_sb")
+        nc.sync.dma_start(offs_sb[:], offs)
+        two_sb = keep.tile([P, S // 16], U16, name="two_sb")
+        nc.sync.dma_start(two_sb[:], two)
+
+        scales = keep.tile([P, T], U8, name="scales", align_bytes=64)
+        nc.vector.memset(scales[:].bitcast(I32), 0)
+        for q in range(4):
+            nc.sync.dma_start(out=scales[32 * q : 32 * q + 4, :].bitcast(I32), in_=x_scales[0, 4 * q : 4 * q + 4, :].bitcast(I32))
+        words = keep.tile([P, T], U32, name="words", align_bytes=64)
+        nc.sync.dma_start(out=words[:].bitcast(I32), in_=x_words[0].rearrange("p c r -> p (c r)").bitcast(I32))
+        load("w2", w2, 0, nc.sync)
+
+        warm_in = keep.tile([P, 1], F32, name="warm_in")
+        nc.vector.memset(warm_in[:], 1.0)
+        warm_out = keep.tile([P, 1], F32, name="warm_out")
+        nc.scalar.activation(out=warm_out[:], in_=warm_in[:], func=ACT.Sqrt)
+
+        n1_sb = keep.tile([P, W // 16], U16, name="n1_sb")
+        nc.sync.dma_start(n1_sb[:], n1)
+        n2_sb = keep.tile([P, W // 16], U16, name="n2_sb")
+        nc.sync.dma_start(n2_sb[:], n2)
+        for c in (1, 2):
+            load("w1", w1, c, nc.sync)
+            load("w2", w2, c, nc.sync)
+
+        picked = {}
+        for name, lst in (("w1", offs_sb), ("w2", two_sb)):
+            sc = keep.tile([P, S], U8, name="picked_scales_" + name, align_bytes=64)
+            nc.vector.tensor_copy(out=sc[:], in_=scales[:].indirect(lst[:]))
+            picked[name, "scales"] = sc
+
+        grouped, codes, planes, accs, hs, pairs, squares, sums, rbs, results = {}, {}, {}, {}, {}, {}, {}, {}, {}, {}
+
+        def group(b, i, copy):
+            name = ("w1", "w2")[i]
+            c = min(b, 2)
+            col = b * P - chunks[c][0]
+            if i == 0:
+                grouped[b] = turns.tile([P, 2 * P * PACK], BF16, name="grouped_%d" % b, align_bytes=64, offset=b * 2048)
+                codes[b] = keep.tile([P, 2 * P], U32, name="codes_%d" % b, align_bytes=64)
+                planes[b] = keep.tile([P, 2 * P], U8, name="plane_%d" % b, align_bytes=64)
+            interleave(copy, grouped[b][:, i * P * PACK : (i + 1) * P * PACK], raw[name, c][:, :, col : col + P])
+
+        def quantize(b, lo, hi):
+            nc.vector.quantize_mx(
+                out=codes[b][:, lo * P : hi * P].bitcast(FP8X4),
+                scales=planes[b][:, lo * P : hi * P],
+                in_=grouped[b][:, lo * P * PACK : hi * P * PACK],
+            )
+
+        def multiply(b):
+            accs[b] = psum.tile([P, S], F32, name="acc_%d" % b)
+            for i, name in enumerate(("w1", "w2")):
+                nc.tensor.matmul_mx(
+                    out=accs[b][:],
+                    lhsT=codes[b][:, i * P : (i + 1) * P].bitcast(FP8X4),
+                    lhsT_scale=planes[b][:, i * P : (i + 1) * P],
+                    rhs=picked[name, "words"][:].bitcast(FP8X4),
+                    rhs_scale=picked[name, "scales"][:],
+                    start=(i == 0),
+                    stop=(i == 1),
+                )
+
+        def fetch(b):
+            hs[b] = keep.tile([P, S], F32, name="h_%d" % b)
+            nc.vector.tensor_copy(out=hs[b][:], in_=accs[b][:])
+            pairs[b] = keep.tile([P, 2 * W], F32, name="pair_%d" % b)
+            nc.scalar.activation(out=pairs[b][:, :W], in_=hs[b][:].indirect(n1_sb[:]), func=ACT.Copy)
+            nc.scalar.activation(out=pairs[b][:, W:], in_=hs[b][:].indirect(n2_sb[:]), func=ACT.Copy)
+
+        def difference(b):
+            pair = pairs[b]
+            rbs[b] = turns.tile([P, W], F32, name="rb_%d" % b, align_bytes=64, offset=(b + 1) * 2048)
+            nc.vector.scalar_tensor_tensor(out=rbs[b][:], in0=pair[:, :W], scalar=-0.5, in1=pair[:, W:], op0=ALU.mult, op1=ALU.add)
+            results[b] = keep.tile([P, S], F32, name="res_%d" % b)
+            nc.scalar.activation(out=results[b][:].indirect(n2_sb[:]), in_=rbs[b][:], func=ACT.Copy)
+            squares[b] = turns.tile([P, 2 * W], F32, name="sq_%d" % b, align_bytes=64, offset=(b + 1) * 2048 + 1024)
+            nc.vector.tensor_tensor(out=squares[b][:], in0=pair[:], in1=pair[:], op=ALU.mult)
+
+        def radicand(b):
+            sums[b] = keep.tile([P, W], F32, name="sum_%d" % b)
+            nc.vector.scalar_tensor_tensor(out=sums[b][:], in0=squares[b][:, :W], scalar=0.25, in1=squares[b][:, W:], op0=ALU.add, op1=ALU.add)
+
+        def root(b):
+            ra = keep.tile([P, W], F32, name="ra_%d" % b)
+            nc.scalar.activation(out=ra[:], in_=sums[b][:], func=ACT.Sqrt)
+            nc.scalar.activation(out=results[b][:].indirect(n1_sb[:]), in_=ra[:], func=ACT.Copy)
+            nc.sync.dma_start(out=out[b * P : (b + 1) * P, :], in_=results[b][:])
+
+        group(0, 0, nc.vector.tensor_copy)
+        quantize(0, 0, 1)
+        for name, lst in (("w1", offs_sb), ("w2", two_sb)):
+            wd = keep.tile([P, S], U32, name="picked_words_" + name, align_bytes=64)
+            nc.vector.tensor_copy(out=wd[:], in_=words[:].indirect(lst[:]))
+            picked[name, "words"] = wd
+        group(0, 1, nc.scalar.copy)
+        quantize(0, 1, 2)
+        multiply(0)
+        group(1, 0, nc.scalar.copy)
+        fetch(0)
+        for b in range(BLOCKS):
+            more = b + 1 < BLOCKS
+            if more:
+                if b > 0:
+                    group(b + 1, 0, nc.vector.tensor_copy)
+                group(b + 1, 1, nc.vector.tensor_copy)
+                quantize(b + 1, 0, 2)
+                multiply(b + 1)
+            difference(b)
+            if more:
+                fetch(b + 1)
+            radicand(b)
+            root(b)

@@ -39,13 +39,16 @@ def tile_picked_ottpolar_none_p_kernel(tc, x_words, x_scales, w1, w2, offs, two,
 
         def load(name, w, c, queue):
             start, width = chunks[c]
-            tile = keep.tile([P, PACK, width], F32, name="raw_%s_%d" % (name, c))
+            if (name, c) == ("w1", 1):
+                tile = turns.tile([P, PACK, width], F32, name="raw_%s_%d" % (name, c), align_bytes=64, offset=24576)
+            else:
+                tile = keep.tile([P, PACK, width], F32, name="raw_%s_%d" % (name, c))
             queue.dma_start(out=tile[:], in_=w.rearrange("(p j) m -> p j m", j=PACK)[:, :, start : start + width])
             raw[name, c] = tile
 
-        load("w1", w1, 0, nc.sync)
         offs_sb = keep.tile([P, S // 16], U16, name="offs_sb")
         nc.sync.dma_start(offs_sb[:], offs)
+        load("w1", w1, 0, nc.sync)
         two_sb = keep.tile([P, S // 16], U16, name="two_sb")
         nc.sync.dma_start(two_sb[:], two)
 
@@ -53,9 +56,9 @@ def tile_picked_ottpolar_none_p_kernel(tc, x_words, x_scales, w1, w2, offs, two,
         nc.vector.memset(scales[:].bitcast(I32), 0)
         for q in range(4):
             nc.sync.dma_start(out=scales[32 * q : 32 * q + 4, :].bitcast(I32), in_=x_scales[0, 4 * q : 4 * q + 4, :].bitcast(I32))
+        load("w2", w2, 0, nc.sync)
         words = keep.tile([P, T], U32, name="words", align_bytes=64)
         nc.sync.dma_start(out=words[:].bitcast(I32), in_=x_words[0].rearrange("p c r -> p (c r)").bitcast(I32))
-        load("w2", w2, 0, nc.sync)
 
         warm_in = keep.tile([P, 1], F32, name="warm_in")
         nc.vector.memset(warm_in[:], 1.0)
@@ -76,32 +79,29 @@ def tile_picked_ottpolar_none_p_kernel(tc, x_words, x_scales, w1, w2, offs, two,
             nc.vector.tensor_copy(out=sc[:], in_=scales[:].indirect(lst[:]))
             picked[name, "scales"] = sc
 
+        ras = {}
         grouped, codes, planes, accs, hs, pairs, squares, sums, rbs, results = {}, {}, {}, {}, {}, {}, {}, {}, {}, {}
 
         def group(b, i, copy):
             name = ("w1", "w2")[i]
             c = min(b, 2)
             col = b * P - chunks[c][0]
-            if i == 0:
-                grouped[b] = turns.tile([P, 2 * P * PACK], BF16, name="grouped_%d" % b, align_bytes=64, offset=b * 2048)
-                codes[b] = keep.tile([P, 2 * P], U32, name="codes_%d" % b, align_bytes=64)
-                planes[b] = keep.tile([P, 2 * P], U8, name="plane_%d" % b, align_bytes=64)
-            interleave(copy, grouped[b][:, i * P * PACK : (i + 1) * P * PACK], raw[name, c][:, :, col : col + P])
+            grouped[b, i] = turns.tile([P, P * PACK], BF16, name="grouped_%d_%d" % (b, i), align_bytes=64, offset=(3 * b + i) * 1024)
+            interleave(copy, grouped[b, i][:], raw[name, c][:, :, col : col + P])
 
-        def quantize(b, lo, hi):
-            nc.vector.quantize_mx(
-                out=codes[b][:, lo * P : hi * P].bitcast(FP8X4),
-                scales=planes[b][:, lo * P : hi * P],
-                in_=grouped[b][:, lo * P * PACK : hi * P * PACK],
-            )
+        def quantize(b, i):
+            place = 4 * 1024 if (b, i) == (0, 1) else 16384 + (2 * b + i) * 512
+            codes[b, i] = turns.tile([P, P], U32, name="codes_%d_%d" % (b, i), align_bytes=64, offset=place)
+            planes[b, i] = keep.tile([P, P], U8, name="plane_%d_%d" % (b, i), align_bytes=64)
+            nc.vector.quantize_mx(out=codes[b, i][:].bitcast(FP8X4), scales=planes[b, i][:], in_=grouped[b, i][:])
 
         def multiply(b):
             accs[b] = psum.tile([P, S], F32, name="acc_%d" % b)
             for i, name in enumerate(("w1", "w2")):
                 nc.tensor.matmul_mx(
                     out=accs[b][:],
-                    lhsT=codes[b][:, i * P : (i + 1) * P].bitcast(FP8X4),
-                    lhsT_scale=planes[b][:, i * P : (i + 1) * P],
+                    lhsT=codes[b, i][:].bitcast(FP8X4),
+                    lhsT_scale=planes[b, i][:],
                     rhs=picked[name, "words"][:].bitcast(FP8X4),
                     rhs_scale=picked[name, "scales"][:],
                     start=(i == 0),
@@ -111,17 +111,17 @@ def tile_picked_ottpolar_none_p_kernel(tc, x_words, x_scales, w1, w2, offs, two,
         def fetch(b):
             hs[b] = keep.tile([P, S], F32, name="h_%d" % b)
             nc.vector.tensor_copy(out=hs[b][:], in_=accs[b][:])
-            pairs[b] = keep.tile([P, 2 * W], F32, name="pair_%d" % b)
+            pairs[b] = turns.tile([P, 2 * W], F32, name="pair_%d" % b, align_bytes=64, offset=24576 + b * 2048)
             nc.scalar.activation(out=pairs[b][:, :W], in_=hs[b][:].indirect(n1_sb[:]), func=ACT.Copy)
             nc.scalar.activation(out=pairs[b][:, W:], in_=hs[b][:].indirect(n2_sb[:]), func=ACT.Copy)
 
         def difference(b):
             pair = pairs[b]
-            rbs[b] = turns.tile([P, W], F32, name="rb_%d" % b, align_bytes=64, offset=(b + 1) * 2048)
+            rbs[b] = turns.tile([P, W], F32, name="rb_%d" % b, align_bytes=64, offset=(3 * b + 4) * 1024)
             nc.vector.scalar_tensor_tensor(out=rbs[b][:], in0=pair[:, :W], scalar=-0.5, in1=pair[:, W:], op0=ALU.mult, op1=ALU.add)
             results[b] = keep.tile([P, S], F32, name="res_%d" % b)
             nc.scalar.activation(out=results[b][:].indirect(n2_sb[:]), in_=rbs[b][:], func=ACT.Copy)
-            squares[b] = turns.tile([P, 2 * W], F32, name="sq_%d" % b, align_bytes=64, offset=(b + 1) * 2048 + 1024)
+            squares[b] = turns.tile([P, 2 * W], F32, name="sq_%d" % b, align_bytes=64, offset=(3 * b + 4) * 1024 + 512)
             nc.vector.tensor_tensor(out=squares[b][:], in0=pair[:], in1=pair[:], op=ALU.mult)
 
         def radicand(b):
@@ -129,19 +129,21 @@ def tile_picked_ottpolar_none_p_kernel(tc, x_words, x_scales, w1, w2, offs, two,
             nc.vector.scalar_tensor_tensor(out=sums[b][:], in0=squares[b][:, :W], scalar=0.25, in1=squares[b][:, W:], op0=ALU.add, op1=ALU.add)
 
         def root(b):
-            ra = keep.tile([P, W], F32, name="ra_%d" % b)
-            nc.scalar.activation(out=ra[:], in_=sums[b][:], func=ACT.Sqrt)
-            nc.scalar.activation(out=results[b][:].indirect(n1_sb[:]), in_=ra[:], func=ACT.Copy)
+            ras[b] = keep.tile([P, W], F32, name="ra_%d" % b)
+            nc.scalar.activation(out=ras[b][:], in_=sums[b][:], func=ACT.Sqrt)
+
+        def put(b):
+            nc.scalar.activation(out=results[b][:].indirect(n1_sb[:]), in_=ras[b][:], func=ACT.Copy)
             nc.sync.dma_start(out=out[b * P : (b + 1) * P, :], in_=results[b][:])
 
         group(0, 0, nc.vector.tensor_copy)
-        quantize(0, 0, 1)
+        quantize(0, 0)
+        group(0, 1, nc.vector.tensor_copy)
+        quantize(0, 1)
         for name, lst in (("w1", offs_sb), ("w2", two_sb)):
             wd = keep.tile([P, S], U32, name="picked_words_" + name, align_bytes=64)
             nc.vector.tensor_copy(out=wd[:], in_=words[:].indirect(lst[:]))
             picked[name, "words"] = wd
-        group(0, 1, nc.scalar.copy)
-        quantize(0, 1, 2)
         multiply(0)
         group(1, 0, nc.scalar.copy)
         fetch(0)
@@ -151,10 +153,12 @@ def tile_picked_ottpolar_none_p_kernel(tc, x_words, x_scales, w1, w2, offs, two,
                 if b > 0:
                     group(b + 1, 0, nc.vector.tensor_copy)
                 group(b + 1, 1, nc.vector.tensor_copy)
-                quantize(b + 1, 0, 2)
+                quantize(b + 1, 0)
+                quantize(b + 1, 1)
                 multiply(b + 1)
             difference(b)
-            if more:
-                fetch(b + 1)
             radicand(b)
             root(b)
+            if more:
+                fetch(b + 1)
+            put(b)

@@ -34,7 +34,7 @@ def tile_picked_ottpolar_none_p_kernel(tc, x_words, x_scales, w1, w2, offs, two,
         turns = ctx.enter_context(tc.tile_pool(name="turns", bufs=1))
         psum = ctx.enter_context(tc.psum_pool(name="psum", bufs=1))
 
-        chunks = [(0, 128), (128, 128), (256, 256)]
+        chunks = [(0, 128), (128, 128), (256, 128), (384, 128)]
         raw = {}
 
         def load(name, w, c, queue):
@@ -69,7 +69,7 @@ def tile_picked_ottpolar_none_p_kernel(tc, x_words, x_scales, w1, w2, offs, two,
         nc.sync.dma_start(n1_sb[:], n1)
         n2_sb = keep.tile([P, W // 16], U16, name="n2_sb")
         nc.sync.dma_start(n2_sb[:], n2)
-        for c in (1, 2):
+        for c in (1, 2, 3):
             load("w1", w1, c, nc.sync)
             load("w2", w2, c, nc.sync)
 
@@ -84,7 +84,7 @@ def tile_picked_ottpolar_none_p_kernel(tc, x_words, x_scales, w1, w2, offs, two,
 
         def group(b, i, copy):
             name = ("w1", "w2")[i]
-            c = min(b, 2)
+            c = b
             col = b * P - chunks[c][0]
             grouped[b, i] = turns.tile([P, P * PACK], BF16, name="grouped_%d_%d" % (b, i), align_bytes=64, offset=(3 * b + i) * 1024)
             interleave(copy, grouped[b, i][:], raw[name, c][:, :, col : col + P])

from contextlib import ExitStack

import concourse.mybir as mybir

K, T, S, N, W = 512, 2048, 256, 512, 128
FLOPS = 2 * 2 * K * N * S

F32 = mybir.dt.float32
BF16 = mybir.dt.bfloat16
I32 = mybir.dt.int32
U32 = mybir.dt.uint32
U16 = mybir.dt.uint16
U8 = mybir.dt.uint8
FP8X4 = mybir.dt.float8_e4m3fn_x4
ACT = mybir.ActivationFunctionType
ALU = mybir.AluOpType

P = 128
PACK = 4
BLOCKS = N // P


def interleave(engine_copy, grouped, raw):
    engine_copy(
        out=grouped.rearrange("p (c i t) -> p c t i", i=4, t=PACK),
        in_=raw.rearrange("p t (c i) -> p c t i", i=4),
    )


def tile_picked_ottpolar_none_p_kernel(tc, x_words, x_scales, w1, w2, offs, two, n1, n2, out):
    nc = tc.nc
    with ExitStack() as ctx:
        keep = ctx.enter_context(tc.tile_pool(name="keep", bufs=1))
        turns = ctx.enter_context(tc.tile_pool(name="turns", bufs=1))
        psum = ctx.enter_context(tc.psum_pool(name="psum", bufs=1))

        chunks = [(0, 128), (128, 128), (256, 128), (384, 128)]
        raw = {}

        def load(name, w, c, queue):
            start, width = chunks[c]
            if (name, c) == ("w1", 1):
                tile = turns.tile([P, PACK, width], F32, name="raw_%s_%d" % (name, c), align_bytes=64, offset=24576)
            else:
                tile = keep.tile([P, PACK, width], F32, name="raw_%s_%d" % (name, c))
            queue.dma_start(out=tile[:], in_=w.rearrange("(p j) m -> p j m", j=PACK)[:, :, start : start + width])
            raw[name, c] = tile

        offs_sb = keep.tile([P, S // 16], U16, name="offs_sb")
        nc.sync.dma_start(offs_sb[:], offs)
        load("w1", w1, 0, nc.sync)
        two_sb = keep.tile([P, S // 16], U16, name="two_sb")
        nc.sync.dma_start(two_sb[:], two)

        scales = keep.tile([P, T], U8, name="scales", align_bytes=64)
        nc.vector.memset(scales[:].bitcast(I32), 0)
        for q in range(4):
            nc.sync.dma_start(out=scales[32 * q : 32 * q + 4, :].bitcast(I32), in_=x_scales[0, 4 * q : 4 * q + 4, :].bitcast(I32))
        load("w2", w2, 0, nc.sync)
        words = keep.tile([P, T], U32, name="words", align_bytes=64)
        nc.sync.dma_start(out=words[:].bitcast(I32), in_=x_words[0].rearrange("p c r -> p (c r)").bitcast(I32))

        warm_in = keep.tile([P, 1], F32, name="warm_in")
        nc.vector.memset(warm_in[:], 1.0)
        warm_out = keep.tile([P, 1], F32, name="warm_out")
        nc.scalar.activation(out=warm_out[:], in_=warm_in[:], func=ACT.Sqrt)

        n1_sb = keep.tile([P, W // 16], U16, name="n1_sb")
        nc.sync.dma_start(n1_sb[:], n1)
        n2_sb = keep.tile([P, W // 16], U16, name="n2_sb")
        nc.sync.dma_start(n2_sb[:], n2)
        for c in (1, 2, 3):
            load("w1", w1, c, nc.sync)
            load("w2", w2, c, nc.sync)

        picked = {}
        for name, lst in (("w1", offs_sb), ("w2", two_sb)):
            sc = keep.tile([P, S], U8, name="picked_scales_" + name, align_bytes=64)
            nc.vector.tensor_copy(out=sc[:], in_=scales[:].indirect(lst[:]))
            picked[name, "scales"] = sc

        ras = {}
        grouped, codes, planes, accs, hs, pairs, squares, sums, rbs, results = {}, {}, {}, {}, {}, {}, {}, {}, {}, {}

        def group(b, i, copy):
            name = ("w1", "w2")[i]
            c = b
            col = b * P - chunks[c][0]
            grouped[b, i] = turns.tile([P, P * PACK], BF16, name="grouped_%d_%d" % (b, i), align_bytes=64, offset=(3 * b + i) * 1024)
            interleave(copy, grouped[b, i][:], raw[name, c][:, :, col : col + P])

        def quantize(b, i):
            place = 4 * 1024 if (b, i) == (0, 1) else 16384 + (2 * b + i) * 512
            codes[b, i] = turns.tile([P, P], U32, name="codes_%d_%d" % (b, i), align_bytes=64, offset=place)
            planes[b, i] = keep.tile([P, P], U8, name="plane_%d_%d" % (b, i), align_bytes=64)
            nc.vector.quantize_mx(out=codes[b, i][:].bitcast(FP8X4), scales=planes[b, i][:], in_=grouped[b, i][:])

        def multiply(b):
            accs[b] = psum.tile([P, S], F32, name="acc_%d" % b)
            for i, name in enumerate(("w1", "w2")):
                nc.tensor.matmul_mx(
                    out=accs[b][:],
                    lhsT=codes[b, i][:].bitcast(FP8X4),
                    lhsT_scale=planes[b, i][:],
                    rhs=picked[name, "words"][:].bitcast(FP8X4),
                    rhs_scale=picked[name, "scales"][:],
                    start=(i == 0),
                    stop=(i == 1),
                )

        def fetch(b):
            hs[b] = keep.tile([P, S], F32, name="h_%d" % b)
            nc.vector.tensor_copy(out=hs[b][:], in_=accs[b][:])
            pairs[b] = turns.tile([P, 2 * W], F32, name="pair_%d" % b, align_bytes=64, offset=24576 + b * 2048)
            nc.scalar.activation(out=pairs[b][:, :W], in_=hs[b][:].indirect(n1_sb[:]), func=ACT.Copy)
            nc.scalar.activation(out=pairs[b][:, W:], in_=hs[b][:].indirect(n2_sb[:]), func=ACT.Copy)

        def difference(b):
            pair = pairs[b]
            rbs[b] = turns.tile([P, W], F32, name="rb_%d" % b, align_bytes=64, offset=(3 * b + 4) * 1024)
            nc.vector.scalar_tensor_tensor(out=rbs[b][:], in0=pair[:, :W], scalar=-0.5, in1=pair[:, W:], op0=ALU.mult, op1=ALU.add)
            results[b] = keep.tile([P, S], F32, name="res_%d" % b)
            nc.scalar.activation(out=results[b][:].indirect(n2_sb[:]), in_=rbs[b][:], func=ACT.Copy)
            squares[b] = turns.tile([P, 2 * W], F32, name="sq_%d" % b, align_bytes=64, offset=(3 * b + 4) * 1024 + 512)
            nc.vector.tensor_tensor(out=squares[b][:], in0=pair[:], in1=pair[:], op=ALU.mult)

        def radicand(b):
            sums[b] = keep.tile([P, W], F32, name="sum_%d" % b)
            nc.vector.scalar_tensor_tensor(out=sums[b][:], in0=squares[b][:, :W], scalar=0.25, in1=squares[b][:, W:], op0=ALU.add, op1=ALU.add)

        def root(b):
            ras[b] = keep.tile([P, W], F32, name="ra_%d" % b)
            nc.scalar.activation(out=ras[b][:], in_=sums[b][:], func=ACT.Sqrt)

        def put(b):
            nc.scalar.activation(out=results[b][:].indirect(n1_sb[:]), in_=ras[b][:], func=ACT.Copy)
            nc.sync.dma_start(out=out[b * P : (b + 1) * P, :], in_=results[b][:])

        group(0, 0, nc.vector.tensor_copy)
        quantize(0, 0)
        group(0, 1, nc.vector.tensor_copy)
        quantize(0, 1)
        for name, lst in (("w1", offs_sb), ("w2", two_sb)):
            wd = keep.tile([P, S], U32, name="picked_words_" + name, align_bytes=64)
            nc.vector.tensor_copy(out=wd[:], in_=words[:].indirect(lst[:]))
            picked[name, "words"] = wd
        multiply(0)
        group(1, 0, nc.scalar.copy)
        fetch(0)
        for b in range(BLOCKS):
            more = b + 1 < BLOCKS
            if more:
                if b > 0:
                    group(b + 1, 0, nc.vector.tensor_copy)
                group(b + 1, 1, nc.vector.tensor_copy)
                quantize(b + 1, 0)
                quantize(b + 1, 1)
                multiply(b + 1)
            difference(b)
            radicand(b)
            root(b)
            if more:
                fetch(b + 1)
            put(b)
